import numpy as np
import ml_dtypes


def mxq(x, axis, fmt="e4m3"):
    dtype, down = {"e4m3": (ml_dtypes.float8_e4m3fn, 7), "e5m2": (ml_dtypes.float8_e5m2, 14)}[fmt]
    v = np.moveaxis(np.asarray(x, np.float32).astype(ml_dtypes.bfloat16).astype(np.float64), axis, -1)
    blocks = v.reshape(v.shape[:-1] + (-1, 32))
    amax = np.abs(blocks).max(-1, keepdims=True)
    byte = np.maximum(np.where(amax > 0, np.frexp(amax)[1] - 1 + 127, 0) - down, 1)
    scale = np.exp2(byte - 127.0)
    codes = (blocks / scale).astype(np.float32).astype(dtype).astype(np.float64)
    return np.moveaxis((codes * scale).reshape(v.shape), -1, axis)


WIDE = False


def mx_kscale(k):
    if not WIDE:
        return np.ones(k)
    levels = np.array([10, -10, 5, -5, 0])
    if k % 512:
        return np.exp2(np.random.permutation(np.resize(levels, k // 32))).repeat(32)
    a = np.empty((k // 512, 16))
    for p in range(k // 512):
        a[p, :8] = np.random.permutation(np.resize(levels, 8))
        for g in range(8):
            far = levels[np.abs(levels - a[p, g]) >= 10]
            a[p, g + 8] = far[np.random.randint(len(far))]
    return np.exp2(a.ravel()).repeat(32)


def f64(x):
    return np.asarray(x).astype(np.float64)


def striped(idx):
    return np.tile(np.asarray(idx).reshape(-1, 16).T, (8, 1)).astype(np.uint16)


def unstriped(offs):
    return offs[:16].T.reshape(-1).astype(np.int64)


E2M1 = np.array([0.0, 0.5, 1.0, 1.5, 2.0, 3.0, 4.0, 6.0, -0.0, -0.5, -1.0, -1.5, -2.0, -3.0, -4.0, -6.0])


def pack_weight(w, fmt):
    k, n = w.shape
    w = f64(np.asarray(w, np.float32).astype(ml_dtypes.bfloat16)).reshape(k // 32, 32, n)
    amax = np.abs(w).max(1)
    if fmt == "e4m3":
        byte = np.frexp(amax)[1] - 1 + 127 - 7
    else:
        mant, ex = np.frexp(amax / 6.0)
        byte = np.where(mant > 0.5, ex, ex - 1) + 127
    byte = np.clip(np.where(amax > 0, byte, 1), 1, 254)
    scaled = (w * np.exp2(127.0 - byte)[:, None, :]).reshape(k, n).astype(np.float32)
    by_word = np.ascontiguousarray(scaled.reshape(k // 512, 128, 4, n).transpose(0, 1, 3, 2))
    if fmt == "e4m3":
        words = by_word.astype(ml_dtypes.float8_e4m3fn).view(np.uint8)
    else:
        c = by_word.astype(ml_dtypes.float4_e2m1fn).view(np.uint8) & 0xF
        words = (c[..., 0::2] | (c[..., 1::2] << 4)).reshape(k // 512, 128, 2 * n)
    return np.ascontiguousarray(words), np.ascontiguousarray(byte.astype(np.uint8).reshape(k // 512, 16, n))


def unpack_weight(words, scales, fmt):
    g, _, n = scales.shape
    words = np.ascontiguousarray(words).reshape(g, 128, n, -1)
    if fmt == "e4m3":
        vals = words.view(ml_dtypes.float8_e4m3fn).astype(np.float64)
    else:
        nib = np.empty((g, 128, n, 4), np.uint8)
        nib[..., 0::2] = words & 0xF
        nib[..., 1::2] = words >> 4
        vals = E2M1[nib]
    vals = vals * np.repeat(np.exp2(scales.astype(np.float64) - 127.0), 8, axis=1)[..., None]
    return vals.transpose(0, 1, 3, 2).reshape(g * 512, n)


D, E, T, I, Q, G = 512, 512, 2048, 512, 128, 32


def setup_inputs():
    n = np.random.standard_normal
    idx = np.random.permutation(T)[:I]
    fd = mx_kscale(D)
    fi = mx_kscale(I)
    ti = np.ones(T)
    ti[idx] = fi
    keysp = pack_weight(n((D, T)) / fd[:, None], "e4m3")
    return {
        "query": (n((D, Q)) * 0.6 / np.sqrt(D) * fd[:, None]).astype(np.float32),
        "dquery": (n((D, Q)) * 1.0 / np.sqrt(D) * fd[:, None]).astype(np.float32),
        "keys_words": keysp[0],
        "keys_scales": keysp[1],
        "trust": (np.random.uniform(0.3, 1.0, (Q, 1))).astype(np.float32),
        "os": (np.random.uniform(4.0, 16.0, (1, I)) * fi).astype(np.float32),
        "vals": (n((E, T)) / ti).astype(np.float32),
        "offs": striped(idx),
    }


def reference(query, dquery, keys_words, keys_scales, trust, os, vals, offs):
    idx = unstriped(offs)
    keysu = unpack_weight(keys_words, keys_scales, "e4m3")
    queryq = mxq(f64(query), 0, "e4m3")
    keysidxg = keysu[:, idx]
    a = queryq.T @ keysidxg
    dqueryq = mxq(f64(dquery), 0, "e4m3")
    ta = dqueryq.T @ keysidxg
    s = a.reshape(Q, G, I // G).mean(axis=2) * f64(trust)
    sr = np.repeat(s, I // G, axis=1)
    b = a - sr
    p = np.exp(b - np.max(b, axis=1, keepdims=True))
    ts = ta.reshape(Q, G, I // G).mean(axis=2) * f64(trust)
    tsr = np.repeat(ts, I // G, axis=1)
    tb = ta - tsr
    tp = tb * p
    tw = (tp - np.sum(tp, axis=1, keepdims=True) * p / np.sum(p, axis=1, keepdims=True)) / np.sum(p, axis=1, keepdims=True)
    wo1 = tw * f64(os)
    wt1 = wo1.T
    vt1 = f64(vals)[:, idx].T
    wt1q = mxq(wt1, 0, "e4m3")
    vt1q = mxq(vt1, 0, "e4m3")
    o = wt1q.T @ vt1q
    return o

@@ -1,0 +1,186 @@
+from contextlib import ExitStack
+
+import concourse.mybir as mybir
+from concourse.masks import make_identity
+
+D, E, T, I, Q, G = 512, 512, 2048, 512, 128, 32
+FLOPS = 2 * Q * I * D * 2 + 2 * Q * E * I
+
+P = 128
+PACK = 4
+PAGE = I // G
+BLOCKS = E // P
+
+F32 = mybir.dt.float32
+BF16 = mybir.dt.bfloat16
+I32 = mybir.dt.int32
+U32 = mybir.dt.uint32
+U16 = mybir.dt.uint16
+U8 = mybir.dt.uint8
+FP8X4 = mybir.dt.float8_e4m3fn_x4
+ALU = mybir.AluOpType
+ACT = mybir.ActivationFunctionType
+AX = mybir.AxisListType
+
+
+def tile_attend_ttpagecentred_kernel(tc, query, dquery, keys_words, keys_scales, trust, slot_factor, vals, offs, out):
+    nc = tc.nc
+    with ExitStack() as ctx:
+        sb = ctx.enter_context(tc.tile_pool(name="sb", bufs=1))
+        ring = ctx.enter_context(tc.tile_pool(name="ring", bufs=2))
+        ps = ctx.enter_context(tc.psum_pool(name="ps", bufs=1))
+        ps2 = ctx.enter_context(tc.psum_pool(name="ps2", bufs=2))
+
+        offsets = sb.tile([P, I // 16], U16, name="offsets")
+        nc.sync.dma_start(offsets[:], offs)
+        key_words = sb.tile([P, T], I32, name="key_words")
+        nc.sync.dma_start(key_words[:], keys_words[0].rearrange("p n t -> p (n t)").bitcast(I32))
+        key_bytes = sb.tile([P, T], U8, name="key_bytes")
+        nc.vector.memset(key_bytes[:].bitcast(I32), 0)
+        for quad in range(4):
+            nc.scalar.dma_start(
+                key_bytes[32 * quad : 32 * quad + 4, :].bitcast(I32),
+                keys_scales[0, 4 * quad : 4 * quad + 4, :].bitcast(I32),
+            )
+        q_raw = []
+        for n, src in enumerate((query, dquery)):
+            raw = sb.tile([P, PACK, Q], F32, name=f"q_raw{n}")
+            nc.sync.dma_start(raw[:], src.rearrange("(p j) w -> p j w", j=PACK))
+            q_raw.append(raw)
+        trust_col = sb.tile([P, 1], F32, name="trust_col")
+        nc.gpsimd.dma_start(trust_col[:], trust)
+        os_cols = sb.tile([P, PACK], F32, name="os_cols")
+        nc.gpsimd.dma_start(os_cols[:], slot_factor.rearrange("o (p t) -> (o p) t", t=PACK))
+        pools = []
+        for j in range(BLOCKS):
+            pool_j = sb.tile([P, T], F32, name=f"vals{j}")
+            nc.sync.dma_start(pool_j[:], vals[j * P : (j + 1) * P, :])
+            pools.append(pool_j)
+
+        warm = sb.tile([P, 1], F32, name="warm")
+        nc.vector.memset(warm[:], 0.0)
+        warm_out = sb.tile([P, 1], F32, name="warm_out")
+        nc.scalar.activation(warm_out[:], warm[:], ACT.Exp)
+
+        ident = sb.tile([P, P], F32, name="ident")
+        make_identity(nc, ident[:])
+
+        k_scales = sb.tile([P, I], U8, name="k_scales", align_bytes=64)
+        nc.vector.tensor_copy(k_scales[:], key_bytes[:].indirect(offsets[:]))
+        k_codes = sb.tile([P, I], U32, name="k_codes", align_bytes=64)
+        nc.vector.tensor_copy(k_codes[:], key_words[:].bitcast(U32).indirect(offsets[:]))
+
+        page_factor = sb.tile([P, 1], F32, name="page_factor")
+        nc.scalar.activation(page_factor[:], trust_col[:], ACT.Copy, scale=1.0 / PAGE)
+
+        scores = []
+        for n in range(2):
+            grouped = sb.tile([P, Q, PACK], BF16, name=f"q_grouped{n}", align_bytes=64)
+            nc.scalar.copy(grouped[:], q_raw[n][:].rearrange("p j w -> p w j"))
+            codes = sb.tile([P, Q], U32, name=f"q_codes{n}", align_bytes=64)
+            scales = sb.tile([P, Q], U8, name=f"q_scales{n}", align_bytes=64)
+            nc.vector.quantize_mx(out=codes[:].bitcast(FP8X4), scales=scales[:], in_=grouped[:].rearrange("p w j -> p (w j)"))
+            acc = ps.tile([P, I], F32, name=f"scores{n}")
+            nc.tensor.matmul_mx(out=acc[:], lhsT=codes[:].bitcast(FP8X4), lhsT_scale=scales[:],
+                                rhs=k_codes[:].bitcast(FP8X4), rhs_scale=k_scales[:], start=True, stop=True)
+            scores.append(acc)
+
+        shifts = []
+        for n in range(2):
+            page_sum = sb.tile([P, G], F32, name=f"page_sum{n}")
+            nc.vector.tensor_reduce(page_sum[:], scores[n][:].rearrange("q (g i) -> q g i", i=PAGE), AX.X, ALU.add)
+            shift = sb.tile([P, G], F32, name=f"shift{n}")
+            nc.scalar.activation(shift[:], page_sum[:], ACT.Copy, scale=page_factor[:])
+            shifts.append(shift)
+
+        centred = []
+        for n in range(2):
+            c = sb.tile([P, PACK, G, PAGE // PACK], F32, name=f"centred{n}")
+            nc.vector.tensor_tensor(
+                c[:],
+                scores[n][:].rearrange("q (g j t) -> q t g j", t=PACK, g=G),
+                shifts[n][:].unsqueeze(1).unsqueeze(3).broadcast_to([P, PACK, G, PAGE // PACK]),
+                ALU.subtract,
+            )
+            centred.append(c[:].rearrange("q t g j -> q (t g j)"))
+        b, tb = centred
+
+        neg_max = sb.tile([P, 1], F32, name="neg_max")
+        nc.vector.tensor_reduce(neg_max[:], b, AX.X, ALU.max, negate=True)
+        p = sb.tile([P, I], F32, name="p")
+        row_sum = sb.tile([P, 1], F32, name="row_sum")
+        nc.scalar.activation(p[:], b, ACT.Exp, bias=neg_max[:], accum_out=row_sum[:])
+
+        v_codes = sb.tile([P, E], U32, name="v_codes", align_bytes=64)
+        v_scales = sb.tile([P, E], U8, name="v_scales", align_bytes=64)
+
+        def gather_values(j):
+            picked = ring.tile([P, I], BF16, name="picked")
+            nc.vector.tensor_copy(picked[:], pools[j][:].indirect(offsets[:]))
+            words = picked[:].bitcast(F32)
+            turned = ps2.tile([P, 2, P], F32, name="turned")
+            for u in range(2):
+                nc.tensor.transpose(turned[:, u, :], words[:, u : I // 2 : 2], ident[:])
+            grouped = ring.tile([P, P * PACK], BF16, name="v_grouped", align_bytes=64)
+            nc.scalar.copy(grouped[:].bitcast(F32).rearrange("p (e u) -> p e u", u=2), turned[:].rearrange("p u e -> p e u"))
+            return grouped
+
+        def quantize_values(j, grouped):
+            cols = slice(j * P, (j + 1) * P)
+            nc.vector.quantize_mx(out=v_codes[:, cols].bitcast(FP8X4), scales=v_scales[:, cols], in_=grouped[:])
+
+        grouped0 = gather_values(0)
+
+        inv_sum = sb.tile([P, 1], F32, name="inv_sum")
+        nc.vector.reciprocal(inv_sum[:], row_sum[:])
+        neg_inv_sum = sb.tile([P, 1], F32, name="neg_inv_sum")
+        nc.scalar.activation(neg_inv_sum[:], inv_sum[:], ACT.Copy, scale=-1.0)
+        tpn = sb.tile([P, I], F32, name="tpn")
+        mean_tb = sb.tile([P, 1], F32, name="mean_tb")
+        quantize_values(0, grouped0)
+        nc.vector.scalar_tensor_tensor(tpn[:], tb, inv_sum[:], p[:], ALU.mult, ALU.mult, accum_out=mean_tb[:])
+        p_factor = sb.tile([P, 1], F32, name="p_factor")
+        nc.scalar.activation(p_factor[:], mean_tb[:], ACT.Copy, scale=neg_inv_sum[:])
+        kp = sb.tile([P, I], F32, name="kp")
+        nc.scalar.activation(kp[:], p[:], ACT.Copy, scale=p_factor[:])
+
+        grouped1 = gather_values(1)
+
+        tw_turned = ps.tile([P, PACK, Q], F32, name="tw_turned")
+        for t in range(PACK):
+            cols = slice(t * P, (t + 1) * P)
+            nc.tensor.matmul(tw_turned[:, t, :], tpn[:, cols], ident[:], start=True, stop=False, is_transpose=True)
+            nc.tensor.matmul(tw_turned[:, t, :], kp[:, cols], ident[:], start=False, stop=True, is_transpose=True)
+        w_grouped = sb.tile([P, Q, PACK], BF16, name="w_grouped", align_bytes=64)
+        nc.vector.tensor_tensor(
+            w_grouped[:],
+            tw_turned[:].rearrange("p t q -> p q t"),
+            os_cols[:].unsqueeze(1).broadcast_to([P, Q, PACK]),
+            ALU.mult,
+        )
+        quantize_values(1, grouped1)
+        w_codes = sb.tile([P, Q], U32, name="w_codes", align_bytes=64)
+        w_scales = sb.tile([P, Q], U8, name="w_scales", align_bytes=64)
+        nc.vector.quantize_mx(out=w_codes[:].bitcast(FP8X4), scales=w_scales[:], in_=w_grouped[:].rearrange("p q t -> p (q t)"))
+
+        def product(acc, first, last):
+            cols = slice(first * P, last * P)
+            nc.tensor.matmul_mx(out=acc, lhsT=w_codes[:].bitcast(FP8X4), lhsT_scale=w_scales[:],
+                                rhs=v_codes[:, cols].bitcast(FP8X4), rhs_scale=v_scales[:, cols], start=True, stop=True)
+
+        def store(acc, first, last, name):
+            result = sb.tile([P, (last - first) * P], F32, name=name)
+            nc.scalar.copy(result[:], acc)
+            nc.sync.dma_start(out[:, first * P : last * P], result[:])
+
+        head = ps.tile([P, 3 * P], F32, name="head")
+        product(head[:, 0 : 2 * P], 0, 2)
+        grouped2 = gather_values(2)
+        quantize_values(2, grouped2)
+        product(head[:, 2 * P : 3 * P], 2, 3)
+        store(head[:], 0, 3, "result_head")
+        grouped3 = gather_values(3)
+        quantize_values(3, grouped3)
+        tail = ps.tile([P, P], F32, name="tail")
+        product(tail[:], 3, 4)
+        store(tail[:], 3, 4, "result_tail")

@@ -27,35 +27,42 @@ def tile_attend_ttpagecentred_kernel(tc, query, dquery, keys_words, keys_scales,
     nc = tc.nc
     with ExitStack() as ctx:
         sb = ctx.enter_context(tc.tile_pool(name="sb", bufs=1))
-        ring = ctx.enter_context(tc.tile_pool(name="ring", bufs=2))
         ps = ctx.enter_context(tc.psum_pool(name="ps", bufs=1))
-        ps2 = ctx.enter_context(tc.psum_pool(name="ps2", bufs=2))
+        ps2 = ctx.enter_context(tc.psum_pool(name="ps2", bufs=3))
+        late = ctx.enter_context(tc.tile_pool(name="late", bufs=1))
+
+        key_bytes = sb.tile([P, T], U8, name="key_bytes")
+        nc.gpsimd.memset(key_bytes[:].bitcast(I32), 0)
 
         offsets = sb.tile([P, I // 16], U16, name="offsets")
         nc.sync.dma_start(offsets[:], offs)
-        key_words = sb.tile([P, T], I32, name="key_words")
-        nc.sync.dma_start(key_words[:], keys_words[0].rearrange("p n t -> p (n t)").bitcast(I32))
-        key_bytes = sb.tile([P, T], U8, name="key_bytes")
-        nc.vector.memset(key_bytes[:].bitcast(I32), 0)
+        trust_col = sb.tile([P, 1], F32, name="trust_col")
+        nc.sync.dma_start(trust_col[:], trust)
+        q_raw = [sb.tile([P, PACK, Q], F32, name=f"q_raw{n}") for n in range(2)]
+        nc.sync.dma_start(q_raw[0][:], query.rearrange("(p j) w -> p j w", j=PACK))
         for quad in range(4):
-            nc.scalar.dma_start(
+            nc.sync.dma_start(
                 key_bytes[32 * quad : 32 * quad + 4, :].bitcast(I32),
                 keys_scales[0, 4 * quad : 4 * quad + 4, :].bitcast(I32),
             )
-        q_raw = []
-        for n, src in enumerate((query, dquery)):
-            raw = sb.tile([P, PACK, Q], F32, name=f"q_raw{n}")
-            nc.sync.dma_start(raw[:], src.rearrange("(p j) w -> p j w", j=PACK))
-            q_raw.append(raw)
-        trust_col = sb.tile([P, 1], F32, name="trust_col")
-        nc.gpsimd.dma_start(trust_col[:], trust)
+        key_words = sb.tile([P, T], I32, name="key_words")
+        nc.sync.dma_start(key_words[:], keys_words[0].rearrange("p n t -> p (n t)").bitcast(I32))
+        nc.sync.dma_start(q_raw[1][:], dquery.rearrange("(p j) w -> p j w", j=PACK))
         os_cols = sb.tile([P, PACK], F32, name="os_cols")
-        nc.gpsimd.dma_start(os_cols[:], slot_factor.rearrange("o (p t) -> (o p) t", t=PACK))
-        pools = []
-        for j in range(BLOCKS):
-            pool_j = sb.tile([P, T], F32, name=f"vals{j}")
-            nc.sync.dma_start(pool_j[:], vals[j * P : (j + 1) * P, :])
-            pools.append(pool_j)
+        halves = []
+        for h in range(4):
+            half = sb.tile([P, T // 4], F32, name=f"vals0_half{h}")
+            nc.sync.dma_start(half[:], vals[0:P, h * (T // 4) : (h + 1) * (T // 4)])
+            halves.append(half)
+        pools = {}
+        for j in range(1, BLOCKS):
+            if j < BLOCKS - 1:
+                pools[j] = sb.tile([P, T], F32, name=f"vals{j}", tag=f"vals{j}", align_bytes=64)
+            else:
+                pools[j] = late.tile([P, T], F32, name=f"vals{j}", offset=0, align_bytes=64)
+            nc.sync.dma_start(pools[j][:], vals[j * P : (j + 1) * P, :])
+            if j == 1:
+                nc.sync.dma_start(os_cols[:], slot_factor.rearrange("o (p t) -> (o p) t", t=PACK))
 
         warm = sb.tile([P, 1], F32, name="warm")
         nc.vector.memset(warm[:], 0.0)
@@ -70,9 +77,6 @@ def tile_attend_ttpagecentred_kernel(tc, query, dquery, keys_words, keys_scales,
         k_codes = sb.tile([P, I], U32, name="k_codes", align_bytes=64)
         nc.vector.tensor_copy(k_codes[:], key_words[:].bitcast(U32).indirect(offsets[:]))
 
-        page_factor = sb.tile([P, 1], F32, name="page_factor")
-        nc.scalar.activation(page_factor[:], trust_col[:], ACT.Copy, scale=1.0 / PAGE)
-
         scores = []
         for n in range(2):
             grouped = sb.tile([P, Q, PACK], BF16, name=f"q_grouped{n}", align_bytes=64)
@@ -80,107 +84,113 @@ def tile_attend_ttpagecentred_kernel(tc, query, dquery, keys_words, keys_scales,
             codes = sb.tile([P, Q], U32, name=f"q_codes{n}", align_bytes=64)
             scales = sb.tile([P, Q], U8, name=f"q_scales{n}", align_bytes=64)
             nc.vector.quantize_mx(out=codes[:].bitcast(FP8X4), scales=scales[:], in_=grouped[:].rearrange("p w j -> p (w j)"))
-            acc = ps.tile([P, I], F32, name=f"scores{n}")
+            acc = ps.tile([P, I], F32, name=f"scores{n}", tag=f"bank{n}")
             nc.tensor.matmul_mx(out=acc[:], lhsT=codes[:].bitcast(FP8X4), lhsT_scale=scales[:],
                                 rhs=k_codes[:].bitcast(FP8X4), rhs_scale=k_scales[:], start=True, stop=True)
             scores.append(acc)
 
-        shifts = []
+        page_sums = []
         for n in range(2):
             page_sum = sb.tile([P, G], F32, name=f"page_sum{n}")
             nc.vector.tensor_reduce(page_sum[:], scores[n][:].rearrange("q (g i) -> q g i", i=PAGE), AX.X, ALU.add)
-            shift = sb.tile([P, G], F32, name=f"shift{n}")
-            nc.scalar.activation(shift[:], page_sum[:], ACT.Copy, scale=page_factor[:])
-            shifts.append(shift)
-
-        centred = []
-        for n in range(2):
-            c = sb.tile([P, PACK, G, PAGE // PACK], F32, name=f"centred{n}")
+            page_sums.append(page_sum)
+        def centre(n):
+            shift = sb.tile([P, G], F32, name=f"shift{n}", tag="shift")
+            nc.vector.tensor_scalar(shift[:], page_sums[n][:], trust_col[:], 1.0 / PAGE, ALU.mult, ALU.mult)
+            centred = sb.tile([P, PACK, G, PAGE // PACK], F32, name=f"centred{n}", tag=f"centred{n}")
             nc.vector.tensor_tensor(
-                c[:],
+                centred[:],
                 scores[n][:].rearrange("q (g j t) -> q t g j", t=PACK, g=G),
-                shifts[n][:].unsqueeze(1).unsqueeze(3).broadcast_to([P, PACK, G, PAGE // PACK]),
+                shift[:].unsqueeze(1).unsqueeze(3).broadcast_to([P, PACK, G, PAGE // PACK]),
                 ALU.subtract,
             )
-            centred.append(c[:].rearrange("q t g j -> q (t g j)"))
-        b, tb = centred
+            return centred[:].rearrange("q t g j -> q (t g j)")
 
+        b = centre(0)
         neg_max = sb.tile([P, 1], F32, name="neg_max")
         nc.vector.tensor_reduce(neg_max[:], b, AX.X, ALU.max, negate=True)
-        p = sb.tile([P, I], F32, name="p")
+        tb = centre(1)
+
+        vals0 = sb.tile([P, T], BF16, name="vals0", tag="p", align_bytes=64)
+        for h in range(4):
+            nc.scalar.copy(vals0[:, h * (T // 4) : (h + 1) * (T // 4)], halves[h][:])
+        picked = {}
+        picked[0] = sb.tile([P, I], BF16, name="picked0")
+        nc.scalar.activation(picked[0][:], vals0[:].indirect(offsets[:]), ACT.Copy)
+
+        p = sb.tile([P, I], F32, name="p", tag="p", align_bytes=64)
         row_sum = sb.tile([P, 1], F32, name="row_sum")
         nc.scalar.activation(p[:], b, ACT.Exp, bias=neg_max[:], accum_out=row_sum[:])
 
-        v_codes = sb.tile([P, E], U32, name="v_codes", align_bytes=64)
-        v_scales = sb.tile([P, E], U8, name="v_scales", align_bytes=64)
+        def gather_values(j, tag):
+            picked[j] = sb.tile([P, I], BF16, name=f"picked{j}", tag=tag)
+            nc.vector.tensor_copy(picked[j][:], pools[j][:].indirect(offsets[:]))
 
-        def gather_values(j):
-            picked = ring.tile([P, I], BF16, name="picked")
-            nc.vector.tensor_copy(picked[:], pools[j][:].indirect(offsets[:]))
-            words = picked[:].bitcast(F32)
-            turned = ps2.tile([P, 2, P], F32, name="turned")
+        def turn_values(j, grouped):
+            words = picked[j][:].bitcast(F32)
+            if j == 1:
+                turned = ps.tile([P, 2, P], F32, name="turned1", tag="bank0")
+            else:
+                turned = ps2.tile([P, 2, P], F32, name="turned")
             for u in range(2):
                 nc.tensor.transpose(turned[:, u, :], words[:, u : I // 2 : 2], ident[:])
-            grouped = ring.tile([P, P * PACK], BF16, name="v_grouped", align_bytes=64)
-            nc.scalar.copy(grouped[:].bitcast(F32).rearrange("p (e u) -> p e u", u=2), turned[:].rearrange("p u e -> p e u"))
-            return grouped
+            nc.scalar.copy(grouped.bitcast(F32).rearrange("p (e u) -> p e u", u=2), turned[:].rearrange("p u e -> p e u"))
 
-        def quantize_values(j, grouped):
-            cols = slice(j * P, (j + 1) * P)
-            nc.vector.quantize_mx(out=v_codes[:, cols].bitcast(FP8X4), scales=v_scales[:, cols], in_=grouped[:])
+        def quantize(grouped, codes, name):
+            scales = sb.tile(list(codes.shape), U8, name=name, align_bytes=64)
+            nc.vector.quantize_mx(out=codes[:].bitcast(FP8X4), scales=scales[:], in_=grouped)
+            return codes, scales
 
-        grouped0 = gather_values(0)
+        grouped_first = sb.tile([P, P * PACK], BF16, name="grouped_first", align_bytes=64)
+        grouped_last = sb.tile([P, P * PACK], BF16, name="grouped_last", align_bytes=64)
 
         inv_sum = sb.tile([P, 1], F32, name="inv_sum")
         nc.vector.reciprocal(inv_sum[:], row_sum[:])
         neg_inv_sum = sb.tile([P, 1], F32, name="neg_inv_sum")
         nc.scalar.activation(neg_inv_sum[:], inv_sum[:], ACT.Copy, scale=-1.0)
+        neg_soft = sb.tile([P, I], F32, name="neg_soft")
+        nc.scalar.activation(neg_soft[:], p[:], ACT.Copy, scale=neg_inv_sum[:])
         tpn = sb.tile([P, I], F32, name="tpn")
         mean_tb = sb.tile([P, 1], F32, name="mean_tb")
-        quantize_values(0, grouped0)
         nc.vector.scalar_tensor_tensor(tpn[:], tb, inv_sum[:], p[:], ALU.mult, ALU.mult, accum_out=mean_tb[:])
-        p_factor = sb.tile([P, 1], F32, name="p_factor")
-        nc.scalar.activation(p_factor[:], mean_tb[:], ACT.Copy, scale=neg_inv_sum[:])
+        turn_values(0, grouped_first[:])
         kp = sb.tile([P, I], F32, name="kp")
-        nc.scalar.activation(kp[:], p[:], ACT.Copy, scale=p_factor[:])
+        nc.scalar.activation(kp[:], neg_soft[:], ACT.Copy, scale=mean_tb[:])
 
-        grouped1 = gather_values(1)
-
-        tw_turned = ps.tile([P, PACK, Q], F32, name="tw_turned")
+        tw_turned = [ps.tile([P, Q], F32, name=f"tw_turned{t}", tag=f"bank{t}") for t in range(PACK)]
         for t in range(PACK):
-            cols = slice(t * P, (t + 1) * P)
-            nc.tensor.matmul(tw_turned[:, t, :], tpn[:, cols], ident[:], start=True, stop=False, is_transpose=True)
-            nc.tensor.matmul(tw_turned[:, t, :], kp[:, cols], ident[:], start=False, stop=True, is_transpose=True)
+            nc.tensor.matmul(tw_turned[t][:], tpn[:, t * P : (t + 1) * P], ident[:], start=True, stop=False, is_transpose=True)
+        w_planes = sb.tile([P, PACK, Q], BF16, name="w_planes", tag="w_planes", align_bytes=64)
+        for t in range(PACK):
+            nc.tensor.matmul(tw_turned[t][:], kp[:, t * P : (t + 1) * P], ident[:], start=False, stop=True, is_transpose=True)
+            nc.scalar.activation(w_planes[:, t, :], tw_turned[t][:], ACT.Copy, scale=os_cols[:, t : t + 1])
         w_grouped = sb.tile([P, Q, PACK], BF16, name="w_grouped", align_bytes=64)
-        nc.vector.tensor_tensor(
-            w_grouped[:],
-            tw_turned[:].rearrange("p t q -> p q t"),
-            os_cols[:].unsqueeze(1).broadcast_to([P, Q, PACK]),
-            ALU.mult,
-        )
-        quantize_values(1, grouped1)
-        w_codes = sb.tile([P, Q], U32, name="w_codes", align_bytes=64)
-        w_scales = sb.tile([P, Q], U8, name="w_scales", align_bytes=64)
-        nc.vector.quantize_mx(out=w_codes[:].bitcast(FP8X4), scales=w_scales[:], in_=w_grouped[:].rearrange("p q t -> p (q t)"))
+        nc.scalar.copy(w_grouped[:], w_planes[:].rearrange("p t q -> p q t"))
 
-        def product(acc, first, last):
-            cols = slice(first * P, last * P)
+        gather_values(1, "centred1")
+        grouped_middle = sb.tile([P, 2 * P * PACK], BF16, name="grouped_middle", tag="w_planes", align_bytes=64)
+        turn_values(1, grouped_middle[:, 0 : P * PACK])
+        gather_values(2, "picked2")
+        turn_values(2, grouped_middle[:, P * PACK : 2 * P * PACK])
+        gather_values(3, "picked3")
+        turn_values(3, grouped_last[:])
+        w_codes, w_scales = quantize(w_grouped[:].rearrange("p q t -> p (q t)"), late.tile([P, Q], U32, name="w_codes", offset=0, align_bytes=64), "w_scales")
+        v_first = quantize(grouped_first[:], late.tile([P, P], U32, name="v_codes_first", offset=512, align_bytes=64), "v_scales_first")
+        v_middle = quantize(grouped_middle[:], late.tile([P, 2 * P], U32, name="v_codes_middle", offset=1024, align_bytes=64), "v_scales_middle")
+        v_last = quantize(grouped_last[:], sb.tile([P, P], U32, name="v_codes_last", align_bytes=64), "v_scales_last")
+
+        def product(acc, values):
             nc.tensor.matmul_mx(out=acc, lhsT=w_codes[:].bitcast(FP8X4), lhsT_scale=w_scales[:],
-                                rhs=v_codes[:, cols].bitcast(FP8X4), rhs_scale=v_scales[:, cols], start=True, stop=True)
+                                rhs=values[0][:].bitcast(FP8X4), rhs_scale=values[1][:], start=True, stop=True)
 
-        def store(acc, first, last, name):
-            result = sb.tile([P, (last - first) * P], F32, name=name)
-            nc.scalar.copy(result[:], acc)
-            nc.sync.dma_start(out[:, first * P : last * P], result[:])
-
-        head = ps.tile([P, 3 * P], F32, name="head")
-        product(head[:, 0 : 2 * P], 0, 2)
-        grouped2 = gather_values(2)
-        quantize_values(2, grouped2)
-        product(head[:, 2 * P : 3 * P], 2, 3)
-        store(head[:], 0, 3, "result_head")
-        grouped3 = gather_values(3)
-        quantize_values(3, grouped3)
-        tail = ps.tile([P, P], F32, name="tail")
-        product(tail[:], 3, 4)
-        store(tail[:], 3, 4, "result_tail")
+        head = ps.tile([P, 3 * P], F32, name="head", tag="bank2")
+        product(head[:, 0:P], v_first)
+        product(head[:, P : 3 * P], v_middle)
+        head_out = sb.tile([P, 3 * P], F32, name="head_out")
+        nc.scalar.copy(head_out[:], head[:])
+        nc.scalar.dma_start(out[:, 0 : 3 * P], head_out[:])
+        tail = ps.tile([P, P], F32, name="tail", tag="bank1")
+        product(tail[:], v_last)
+        tail_out = sb.tile([P, P], F32, name="tail_out")
+        nc.vector.tensor_copy(tail_out[:], tail[:])
+        nc.sync.dma_start(out[:, 3 * P : E], tail_out[:])

@@ -64,11 +64,6 @@ def tile_attend_ttpagecentred_kernel(tc, query, dquery, keys_words, keys_scales,
             if j == 1:
                 nc.sync.dma_start(os_cols[:], slot_factor.rearrange("o (p t) -> (o p) t", t=PACK))
 
-        warm = sb.tile([P, 1], F32, name="warm")
-        nc.vector.memset(warm[:], 0.0)
-        warm_out = sb.tile([P, 1], F32, name="warm_out")
-        nc.scalar.activation(warm_out[:], warm[:], ACT.Exp)
-
         ident = sb.tile([P, P], F32, name="ident")
         make_identity(nc, ident[:])
 

from contextlib import ExitStack

import concourse.mybir as mybir
from concourse.masks import make_identity

D, E, T, I, Q, G = 512, 512, 2048, 512, 128, 32
FLOPS = 2 * Q * I * D * 2 + 2 * Q * E * I

P = 128
PACK = 4
PAGE = I // G
BLOCKS = E // P

F32 = mybir.dt.float32
BF16 = mybir.dt.bfloat16
I32 = mybir.dt.int32
U32 = mybir.dt.uint32
U16 = mybir.dt.uint16
U8 = mybir.dt.uint8
FP8X4 = mybir.dt.float8_e4m3fn_x4
ALU = mybir.AluOpType
ACT = mybir.ActivationFunctionType
AX = mybir.AxisListType


def tile_attend_ttpagecentred_kernel(tc, query, dquery, keys_words, keys_scales, trust, slot_factor, vals, offs, out):
    nc = tc.nc
    with ExitStack() as ctx:
        sb = ctx.enter_context(tc.tile_pool(name="sb", bufs=1))
        ps = ctx.enter_context(tc.psum_pool(name="ps", bufs=1))
        ps2 = ctx.enter_context(tc.psum_pool(name="ps2", bufs=3))
        late = ctx.enter_context(tc.tile_pool(name="late", bufs=1))

        key_bytes = sb.tile([P, T], U8, name="key_bytes")
        nc.gpsimd.memset(key_bytes[:].bitcast(I32), 0)

        offsets = sb.tile([P, I // 16], U16, name="offsets")
        nc.sync.dma_start(offsets[:], offs)
        trust_col = sb.tile([P, 1], F32, name="trust_col")
        nc.sync.dma_start(trust_col[:], trust)
        q_raw = [sb.tile([P, PACK, Q], F32, name=f"q_raw{n}") for n in range(2)]
        nc.sync.dma_start(q_raw[0][:], query.rearrange("(p j) w -> p j w", j=PACK))
        for quad in range(4):
            nc.sync.dma_start(
                key_bytes[32 * quad : 32 * quad + 4, :].bitcast(I32),
                keys_scales[0, 4 * quad : 4 * quad + 4, :].bitcast(I32),
            )
        key_words = sb.tile([P, T], I32, name="key_words")
        nc.sync.dma_start(key_words[:], keys_words[0].rearrange("p n t -> p (n t)").bitcast(I32))
        nc.sync.dma_start(q_raw[1][:], dquery.rearrange("(p j) w -> p j w", j=PACK))
        os_cols = sb.tile([P, PACK], F32, name="os_cols")
        halves = []
        for h in range(4):
            half = sb.tile([P, T // 4], F32, name=f"vals0_half{h}")
            nc.sync.dma_start(half[:], vals[0:P, h * (T // 4) : (h + 1) * (T // 4)])
            halves.append(half)
        pools = {}
        for j in range(1, BLOCKS):
            if j < BLOCKS - 1:
                pools[j] = sb.tile([P, T], F32, name=f"vals{j}", tag=f"vals{j}", align_bytes=64)
            else:
                pools[j] = late.tile([P, T], F32, name=f"vals{j}", offset=0, align_bytes=64)
            nc.sync.dma_start(pools[j][:], vals[j * P : (j + 1) * P, :])
            if j == 1:
                nc.sync.dma_start(os_cols[:], slot_factor.rearrange("o (p t) -> (o p) t", t=PACK))

        ident = sb.tile([P, P], F32, name="ident")
        make_identity(nc, ident[:])

        k_scales = sb.tile([P, I], U8, name="k_scales", align_bytes=64)
        nc.vector.tensor_copy(k_scales[:], key_bytes[:].indirect(offsets[:]))
        k_codes = sb.tile([P, I], U32, name="k_codes", align_bytes=64)
        nc.vector.tensor_copy(k_codes[:], key_words[:].bitcast(U32).indirect(offsets[:]))

        scores = []
        for n in range(2):
            grouped = sb.tile([P, Q, PACK], BF16, name=f"q_grouped{n}", align_bytes=64)
            nc.scalar.copy(grouped[:], q_raw[n][:].rearrange("p j w -> p w j"))
            codes = sb.tile([P, Q], U32, name=f"q_codes{n}", align_bytes=64)
            scales = sb.tile([P, Q], U8, name=f"q_scales{n}", align_bytes=64)
            nc.vector.quantize_mx(out=codes[:].bitcast(FP8X4), scales=scales[:], in_=grouped[:].rearrange("p w j -> p (w j)"))
            acc = ps.tile([P, I], F32, name=f"scores{n}", tag=f"bank{n}")
            nc.tensor.matmul_mx(out=acc[:], lhsT=codes[:].bitcast(FP8X4), lhsT_scale=scales[:],
                                rhs=k_codes[:].bitcast(FP8X4), rhs_scale=k_scales[:], start=True, stop=True)
            scores.append(acc)

        page_sums = []
        for n in range(2):
            page_sum = sb.tile([P, G], F32, name=f"page_sum{n}")
            nc.vector.tensor_reduce(page_sum[:], scores[n][:].rearrange("q (g i) -> q g i", i=PAGE), AX.X, ALU.add)
            page_sums.append(page_sum)
        def centre(n):
            shift = sb.tile([P, G], F32, name=f"shift{n}", tag="shift")
            nc.vector.tensor_scalar(shift[:], page_sums[n][:], trust_col[:], 1.0 / PAGE, ALU.mult, ALU.mult)
            centred = sb.tile([P, PACK, G, PAGE // PACK], F32, name=f"centred{n}", tag=f"centred{n}")
            nc.vector.tensor_tensor(
                centred[:],
                scores[n][:].rearrange("q (g j t) -> q t g j", t=PACK, g=G),
                shift[:].unsqueeze(1).unsqueeze(3).broadcast_to([P, PACK, G, PAGE // PACK]),
                ALU.subtract,
            )
            return centred[:].rearrange("q t g j -> q (t g j)")

        b = centre(0)
        neg_max = sb.tile([P, 1], F32, name="neg_max")
        nc.vector.tensor_reduce(neg_max[:], b, AX.X, ALU.max, negate=True)
        tb = centre(1)

        vals0 = sb.tile([P, T], BF16, name="vals0", tag="p", align_bytes=64)
        for h in range(4):
            nc.scalar.copy(vals0[:, h * (T // 4) : (h + 1) * (T // 4)], halves[h][:])
        picked = {}
        picked[0] = sb.tile([P, I], BF16, name="picked0")
        nc.scalar.activation(picked[0][:], vals0[:].indirect(offsets[:]), ACT.Copy)

        p = sb.tile([P, I], F32, name="p", tag="p", align_bytes=64)
        row_sum = sb.tile([P, 1], F32, name="row_sum")
        nc.scalar.activation(p[:], b, ACT.Exp, bias=neg_max[:], accum_out=row_sum[:])

        def gather_values(j, tag):
            picked[j] = sb.tile([P, I], BF16, name=f"picked{j}", tag=tag)
            nc.vector.tensor_copy(picked[j][:], pools[j][:].indirect(offsets[:]))

        def turn_values(j, grouped):
            words = picked[j][:].bitcast(F32)
            if j == 1:
                turned = ps.tile([P, 2, P], F32, name="turned1", tag="bank0")
            else:
                turned = ps2.tile([P, 2, P], F32, name="turned")
            for u in range(2):
                nc.tensor.transpose(turned[:, u, :], words[:, u : I // 2 : 2], ident[:])
            nc.scalar.copy(grouped.bitcast(F32).rearrange("p (e u) -> p e u", u=2), turned[:].rearrange("p u e -> p e u"))

        def quantize(grouped, codes, name):
            scales = sb.tile(list(codes.shape), U8, name=name, align_bytes=64)
            nc.vector.quantize_mx(out=codes[:].bitcast(FP8X4), scales=scales[:], in_=grouped)
            return codes, scales

        grouped_first = sb.tile([P, P * PACK], BF16, name="grouped_first", align_bytes=64)
        grouped_last = sb.tile([P, P * PACK], BF16, name="grouped_last", align_bytes=64)

        inv_sum = sb.tile([P, 1], F32, name="inv_sum")
        nc.vector.reciprocal(inv_sum[:], row_sum[:])
        neg_inv_sum = sb.tile([P, 1], F32, name="neg_inv_sum")
        nc.scalar.activation(neg_inv_sum[:], inv_sum[:], ACT.Copy, scale=-1.0)
        neg_soft = sb.tile([P, I], F32, name="neg_soft")
        nc.scalar.activation(neg_soft[:], p[:], ACT.Copy, scale=neg_inv_sum[:])
        tpn = sb.tile([P, I], F32, name="tpn")
        mean_tb = sb.tile([P, 1], F32, name="mean_tb")
        nc.vector.scalar_tensor_tensor(tpn[:], tb, inv_sum[:], p[:], ALU.mult, ALU.mult, accum_out=mean_tb[:])
        turn_values(0, grouped_first[:])
        kp = sb.tile([P, I], F32, name="kp")
        nc.scalar.activation(kp[:], neg_soft[:], ACT.Copy, scale=mean_tb[:])

        tw_turned = [ps.tile([P, Q], F32, name=f"tw_turned{t}", tag=f"bank{t}") for t in range(PACK)]
        for t in range(PACK):
            nc.tensor.matmul(tw_turned[t][:], tpn[:, t * P : (t + 1) * P], ident[:], start=True, stop=False, is_transpose=True)
        w_planes = sb.tile([P, PACK, Q], BF16, name="w_planes", tag="w_planes", align_bytes=64)
        for t in range(PACK):
            nc.tensor.matmul(tw_turned[t][:], kp[:, t * P : (t + 1) * P], ident[:], start=False, stop=True, is_transpose=True)
            nc.scalar.activation(w_planes[:, t, :], tw_turned[t][:], ACT.Copy, scale=os_cols[:, t : t + 1])
        w_grouped = sb.tile([P, Q, PACK], BF16, name="w_grouped", align_bytes=64)
        nc.scalar.copy(w_grouped[:], w_planes[:].rearrange("p t q -> p q t"))

        gather_values(1, "centred1")
        grouped_middle = sb.tile([P, 2 * P * PACK], BF16, name="grouped_middle", tag="w_planes", align_bytes=64)
        turn_values(1, grouped_middle[:, 0 : P * PACK])
        gather_values(2, "picked2")
        turn_values(2, grouped_middle[:, P * PACK : 2 * P * PACK])
        gather_values(3, "picked3")
        turn_values(3, grouped_last[:])
        w_codes, w_scales = quantize(w_grouped[:].rearrange("p q t -> p (q t)"), late.tile([P, Q], U32, name="w_codes", offset=0, align_bytes=64), "w_scales")
        v_first = quantize(grouped_first[:], late.tile([P, P], U32, name="v_codes_first", offset=512, align_bytes=64), "v_scales_first")
        v_middle = quantize(grouped_middle[:], late.tile([P, 2 * P], U32, name="v_codes_middle", offset=1024, align_bytes=64), "v_scales_middle")
        v_last = quantize(grouped_last[:], sb.tile([P, P], U32, name="v_codes_last", align_bytes=64), "v_scales_last")

        def product(acc, values):
            nc.tensor.matmul_mx(out=acc, lhsT=w_codes[:].bitcast(FP8X4), lhsT_scale=w_scales[:],
                                rhs=values[0][:].bitcast(FP8X4), rhs_scale=values[1][:], start=True, stop=True)

        head = ps.tile([P, 3 * P], F32, name="head", tag="bank2")
        product(head[:, 0:P], v_first)
        product(head[:, P : 3 * P], v_middle)
        head_out = sb.tile([P, 3 * P], F32, name="head_out")
        nc.scalar.copy(head_out[:], head[:])
        nc.scalar.dma_start(out[:, 0 : 3 * P], head_out[:])
        tail = ps.tile([P, P], F32, name="tail", tag="bank1")
        product(tail[:], v_last)
        tail_out = sb.tile([P, P], F32, name="tail_out")
        nc.vector.tensor_copy(tail_out[:], tail[:])
        nc.sync.dma_start(out[:, 3 * P : E], tail_out[:])
